import numpy as np
CORES = [6,14,30,38,62,70,86,94,102]
N = 9
TK = 512
CNT = [512,384,512,128,448,128,64,64,256]
NT = sum(CNT)
EPS = 0.01
def setup_inputs(rng):
    return {"x": rng.standard_normal((N, 128, TK), dtype=np.float32) * (0.5 + np.arange(N, dtype=np.float32).reshape(N, 1, 1) / N) + rng.standard_normal((N, 128, 1), dtype=np.float32)}
def setup_inputs_big(rng):
    d = setup_inputs(rng)
    for k in ("x",): d[k] = (d[k].astype(np.float32) * 1024.0).astype(d[k].dtype)
    return d
def setup_inputs_small(rng):
    d = setup_inputs(rng)
    for k in ("x",): d[k] = (d[k].astype(np.float32) * (1 / 1024.0)).astype(d[k].dtype)
    return d
def setup_inputs_apart(rng):
    d = setup_inputs(rng)
    f = (10.0 ** rng.permutation(np.linspace(-1.5, 1.5, N))).astype(np.float32).reshape(N, 1, 1)
    for k in ("x",): d[k] = (d[k].astype(np.float32) * f).astype(d[k].dtype)
    return d
def setup_inputs_mixed(rng):
    d = setup_inputs(rng)
    f = (10.0 ** rng.uniform(-3, 3, (1, 128, 1))).astype(np.float32); shape = rng.integers(3, size=(1, 128, 1))
    for k in ("x",):
        x = d[k].astype(np.float32)
        m = x.mean(axis=(0, 2), keepdims=True); level = m + np.sign(x - m) * np.abs(x - m).mean(axis=(0, 2), keepdims=True) * rng.uniform(0.9, 1.1, x.shape).astype(np.float32)
        other = x * np.where(rng.random(x.shape) < 0.5, 0.1, 1.0).astype(np.float32)
        d[k] = (np.where(shape == 1, level, np.where(shape == 2, other, x)) * f).astype(d[k].dtype)
    return d
def setup_inputs_offset(rng):
    d = setup_inputs(rng)
    x = d["x"]; spread = x.std(axis=(0, 2), keepdims=True)
    d["x"] = (x + spread * rng.uniform(16, 48, (1, 128, 1)) * rng.choice([-1.0, 1.0], (1, 128, 1))).astype(np.float32)
    return d
def reference(x):
    X = x.astype(np.float64); ok = np.arange(TK).reshape(1, 1, TK) < np.array(CNT).reshape(N, 1, 1)
    mu = (X * ok).sum(axis=(0, 2)).reshape(1, 128, 1) / NT
    rs = 1.0 / np.sqrt((((X - mu) ** 2) * ok).sum(axis=(0, 2)).reshape(1, 128, 1) / NT + EPS)
    return {"y": np.where(ok, (X - mu) * rs, np.nan).astype(np.float32)}

@@ -1,0 +1,155 @@
+import math
+from concourse.bass import DstId, RemoteDMATransfer
+from concourse.mybir import AluOpType, AxisListType, ActivationFunctionType
+
+EPS = 0.01
+MAXP = 8
+NE = 8
+TIERS = 3
+
+SCRATCH = {
+    "xb": ("sbuf", [128, 512], "float32"),
+    "yb": ("sbuf", [128, 512], "float32"),
+    "junk": ("sbuf", [128, 512], "float32"),
+    "junk2": ("sbuf", [128, 160], "float32"),
+    "land": ("sbuf", [128, 160], "float32"),
+    "mine": ("sbuf", [128, 16], "float32"),
+    "sm": ("sbuf", [128, 8], "float32"),
+}
+SEMAPHORES = ["ld", "aq", "arr", "snt", "cp", "a0", "a1", "a2", "a3", "v1", "v2", "v3", "vy", "ay", "st"] + \
+             ["vr%d" % j for j in range(MAXP)]
+
+
+def _layout(cnt):
+    n = len(cnt)
+    w = math.gcd(*cnt)
+    k = [c // w for c in cnt]
+    order = [r for r in range(n) if k[r] % 2 == 0] + sorted([r for r in range(n) if k[r] % 2], key=lambda r: k[r])
+    off, p = {}, 0
+    for r in order:
+        off[r] = p
+        p += k[r]
+    return w, k, off, p
+
+
+def _plan(s, cnt, cores, topo):
+    n = len(cnt)
+    top = max(cnt)
+    dests = sorted([d for d in range(n) if d != s], key=lambda d: (-cnt[d], (d - s) % n))
+
+    def tier(d):
+        if TIERS == 1:
+            return 0
+        if TIERS >= n:
+            return dests.index(d)
+        return 0 if cnt[d] == top else (1 if 2 * cnt[d] >= top or TIERS == 2 else 2)
+
+    calls = []
+    for t in sorted(set(tier(d) for d in dests)):
+        grp = [d for d in dests if tier(d) == t]
+        m = -1
+        for d in grp:
+            if not topo.may_write(cores[s], cores[d]):
+                raise ValueError("rank %d may not write to rank %d" % (s, d))
+            m &= topo.mask(cores[s], cores[d])
+        bits = [b for b in range(16) if (m >> b) & 1]
+        e = 1
+        while e * 2 <= min(len(bits), NE):
+            e *= 2
+        calls.append((sum(1 << b for b in bits[:e]), e, grp))
+    return calls
+
+
+def rank_program(g, core, T, topo):
+    rank = T.rank_of(core)
+    if rank is None:
+        return
+    cnt = [int(c) for c in T.tables["CNT"]]
+    cores = [int(c) for c in T.cores]
+    nr = len(cnt)
+    nt = sum(cnt)
+    w, k, off, npair = _layout(cnt)
+    n, kk, o = cnt[rank], k[rank], off[rank]
+    sem = T.sem
+    v, a, s = g.vector, g.scalar, g.sync
+    add, mult = AluOpType.add, AluOpType.mult
+    X = AxisListType.X
+    F = ActivationFunctionType
+
+    direct = o % 2 == 0 and ((o + kk) % 2 == 0 or o + kk == npair)
+    stat, base = (T.land, 2 * o) if direct else (T.mine, 0)
+    slot = T.land[:, 2 * o:2 * (o + kk)]
+    calls = _plan(rank, cnt, cores, topo)
+    arrive = sum(e for q in range(nr) if q != rank for (_, e, grp) in _plan(q, cnt, cores, topo) if rank in grp)
+
+    s.dma_start(T.xb[:, 0:n], T.x[:, 0:n]).then_inc(sem.ld, 16)
+    v.wait_ge(sem.ld, 16)
+    a.wait_ge(sem.ld, 16)
+
+    for j in range(kk):
+        A = stat[:, base + 2 * j:base + 2 * j + 1]
+        Q = stat[:, base + 2 * j + 1:base + 2 * j + 2]
+        xs = T.xb[:, j * w:(j + 1) * w]
+        v.tensor_reduce(A, xs, X, add, negate=True).then_inc(sem["vr%d" % j], 1)
+        a.wait_ge(sem["vr%d" % j], 1)
+        a.activation(T.junk[:, j * w:(j + 1) * w], xs, F.Square, bias=A, scale=float(w), accum_out=Q).then_inc(sem.aq, 1)
+
+    for j in range(kk):
+        g.wait_ge(sem["vr%d" % j], 1)
+    g.wait_ge(sem.aq, kk)
+    sent = 0
+    for (m, e, grp) in calls:
+        ids = []
+        for d in grp:
+            rid, pid, _ = topo.addr(cores[d])
+            ids.append(DstId(rid=rid, pnc=pid))
+        g.remote_dma_fused([RemoteDMATransfer(dst_ids=ids, dma_engine_mask=m, remote_sem=sem.arr,
+                                              srcs=[stat[:, base:base + 2 * kk]], dsts=[slot for _ in grp])],
+                           local_sem=sem.snt)
+        sent += e
+
+    landA = T.land[:, 0:2 * npair:2]
+    landQ = T.land[:, 1:2 * npair:2]
+    tot, qe, bt, sd, rs, negmu, nb = [T.sm[:, i:i + 1] for i in range(7)]
+    for j in range(kk):
+        v.wait_ge(sem["vr%d" % j], 1)
+    v.wait_ge(sem.aq, kk)
+    v.wait_ge(sem.arr, arrive)
+    a.wait_ge(sem.aq, kk)
+    a.wait_ge(sem.arr, arrive)
+    if not direct:
+        v.tensor_copy(slot, T.mine[:, 0:2 * kk]).then_inc(sem.cp, 1)
+        v.wait_ge(sem.cp, 1)
+        a.wait_ge(sem.cp, 1)
+    v.tensor_reduce(tot, landA, X, add, negate=True).then_inc(sem.v1, 1)
+    a.activation(T.junk2[:, 0:npair], landQ, F.Identity, bias=EPS / npair, scale=1.0 / (float(w) * w * nt),
+                 accum_out=qe).then_inc(sem.a0, 1)
+    a.wait_ge(sem.v1, 1)
+    a.activation(T.junk2[:, 80:80 + npair], landA, F.Square, bias=tot, scale=float(npair),
+                 accum_out=bt).then_inc(sem.a1, 1)
+    v.wait_ge(sem.v1, 1)
+    v.tensor_scalar(negmu, tot, -1.0 / nt, None, mult).then_inc(sem.v2, 1)
+    a.wait_ge(sem.a0, 1)
+    a.wait_ge(sem.a1, 1)
+    a.activation(sd, bt, F.Sqrt, bias=qe, scale=float(w) / (float(nt) ** 3)).then_inc(sem.a2, 1)
+    v.wait_ge(sem.a2, 1)
+    v.reciprocal(rs, sd).then_inc(sem.v3, 1)
+
+    na = ((n - w) // 2) // 4 * 4
+    if na < 32:
+        na = 0
+    nv = n - na
+    v.wait_ge(sem.v2, 1)
+    v.wait_ge(sem.v3, 1)
+    v.tensor_scalar(T.yb[:, 0:nv], T.xb[:, 0:nv], negmu, rs, add, mult).then_inc(sem.vy, 1)
+    s.wait_ge(sem.vy, 1)
+    if na:
+        a.wait_ge(sem.v2, 1)
+        a.wait_ge(sem.v3, 1)
+        a.activation(nb, negmu, F.Identity, scale=rs).then_inc(sem.a3, 1)
+        a.wait_ge(sem.a3, 1)
+        a.activation(T.yb[:, nv:n], T.xb[:, nv:n], F.Identity, bias=nb, scale=rs).then_inc(sem.ay, 1)
+        s.wait_ge(sem.ay, 1)
+    s.dma_start(T.y[:, 0:n], T.yb[:, 0:n]).then_inc(sem.st, 16)
+    s.wait_ge(sem.st, 16)
+    g.wait_ge(sem.snt, sent)

@@ -5,7 +5,7 @@ from concourse.mybir import AluOpType, AxisListType, ActivationFunctionType
 EPS = 0.01
 MAXP = 8
 NE = 8
-TIERS = 3
+EARLY = 1
 
 SCRATCH = {
     "xb": ("sbuf", [128, 512], "float32"),
@@ -16,8 +16,8 @@ SCRATCH = {
     "mine": ("sbuf", [128, 16], "float32"),
     "sm": ("sbuf", [128, 8], "float32"),
 }
-SEMAPHORES = ["ld", "aq", "arr", "snt", "cp", "a0", "a1", "a2", "a3", "v1", "v2", "v3", "vy", "ay", "st"] + \
-             ["vr%d" % j for j in range(MAXP)]
+SEMAPHORES = ["ld0", "ld1", "ld2", "ae", "aq", "arr", "snt", "cp", "a0", "a1", "a2", "a3", "v1", "v2", "v3", "vy", "ay",
+              "st"] + ["vr%d" % j for j in range(MAXP)]
 
 
 def _layout(cnt):
@@ -32,21 +32,20 @@ def _layout(cnt):
     return w, k, off, p
 
 
-def _plan(s, cnt, cores, topo):
+def _parts(kk):
+    if kk <= EARLY:
+        return [0]
+    if kk < 4:
+        return [0, EARLY]
+    return [0, EARLY, kk - kk // 4]
+
+
+def _plan(s, cnt, k, cores, topo):
     n = len(cnt)
-    top = max(cnt)
     dests = sorted([d for d in range(n) if d != s], key=lambda d: (-cnt[d], (d - s) % n))
+    ne = EARLY if k[s] > EARLY else 0
 
-    def tier(d):
-        if TIERS == 1:
-            return 0
-        if TIERS >= n:
-            return dests.index(d)
-        return 0 if cnt[d] == top else (1 if 2 * cnt[d] >= top or TIERS == 2 else 2)
-
-    calls = []
-    for t in sorted(set(tier(d) for d in dests)):
-        grp = [d for d in dests if tier(d) == t]
+    def engines(grp):
         m = -1
         for d in grp:
             if not topo.may_write(cores[s], cores[d]):
@@ -56,8 +55,13 @@ def _plan(s, cnt, cores, topo):
         e = 1
         while e * 2 <= min(len(bits), NE):
             e *= 2
-        calls.append((sum(1 << b for b in bits[:e]), e, grp))
-    return calls
+        return sum(1 << b for b in bits[:e]), e
+
+    if not ne:
+        return 0, [engines(dests) + (dests, 0, k[s])]
+    return ne, [engines(dests[-1:]) + (dests[-1:], 0, ne),
+                engines(dests[:-1]) + (dests[:-1], 0, k[s]),
+                engines(dests[-1:]) + (dests[-1:], ne, k[s])]
 
 
 def rank_program(g, core, T, topo):
@@ -78,33 +82,43 @@ def rank_program(g, core, T, topo):
 
     direct = o % 2 == 0 and ((o + kk) % 2 == 0 or o + kk == npair)
     stat, base = (T.land, 2 * o) if direct else (T.mine, 0)
-    slot = T.land[:, 2 * o:2 * (o + kk)]
-    calls = _plan(rank, cnt, cores, topo)
-    arrive = sum(e for q in range(nr) if q != rank for (_, e, grp) in _plan(q, cnt, cores, topo) if rank in grp)
+    ne, calls = _plan(rank, cnt, k, cores, topo)
+    arrive = sum(c[1] for q in range(nr) if q != rank for c in _plan(q, cnt, k, cores, topo)[1] if rank in c[2])
 
-    s.dma_start(T.xb[:, 0:n], T.x[:, 0:n]).then_inc(sem.ld, 16)
-    v.wait_ge(sem.ld, 16)
-    a.wait_ge(sem.ld, 16)
+    parts = _parts(kk)
+    for i, p0 in enumerate(parts):
+        p1 = parts[i + 1] if i + 1 < len(parts) else kk
+        s.dma_start(T.xb[:, p0 * w:p1 * w], T.x[:, p0 * w:p1 * w]).then_inc(sem["ld%d" % i], 16)
 
     for j in range(kk):
+        if j in parts:
+            v.wait_ge(sem["ld%d" % parts.index(j)], 16)
+            a.wait_ge(sem["ld%d" % parts.index(j)], 16)
         A = stat[:, base + 2 * j:base + 2 * j + 1]
         Q = stat[:, base + 2 * j + 1:base + 2 * j + 2]
         xs = T.xb[:, j * w:(j + 1) * w]
         v.tensor_reduce(A, xs, X, add, negate=True).then_inc(sem["vr%d" % j], 1)
         a.wait_ge(sem["vr%d" % j], 1)
-        a.activation(T.junk[:, j * w:(j + 1) * w], xs, F.Square, bias=A, scale=float(w), accum_out=Q).then_inc(sem.aq, 1)
+        a.activation(T.junk[:, j * w:(j + 1) * w], xs, F.Square, bias=A, scale=float(w),
+                     accum_out=Q).then_inc(sem.ae if j < ne else sem.aq, 1)
 
-    for j in range(kk):
-        g.wait_ge(sem["vr%d" % j], 1)
-    g.wait_ge(sem.aq, kk)
     sent = 0
-    for (m, e, grp) in calls:
+    for i, (m, e, grp, p0, p1) in enumerate(calls):
+        if i == 0 and ne:
+            for j in range(ne):
+                g.wait_ge(sem["vr%d" % j], 1)
+            g.wait_ge(sem.ae, ne)
+        if i == (1 if ne else 0):
+            for j in range(ne, kk):
+                g.wait_ge(sem["vr%d" % j], 1)
+            g.wait_ge(sem.aq, kk - ne)
         ids = []
         for d in grp:
             rid, pid, _ = topo.addr(cores[d])
             ids.append(DstId(rid=rid, pnc=pid))
         g.remote_dma_fused([RemoteDMATransfer(dst_ids=ids, dma_engine_mask=m, remote_sem=sem.arr,
-                                              srcs=[stat[:, base:base + 2 * kk]], dsts=[slot for _ in grp])],
+                                              srcs=[stat[:, base + 2 * p0:base + 2 * p1]],
+                                              dsts=[T.land[:, 2 * (o + p0):2 * (o + p1)] for _ in grp])],
                            local_sem=sem.snt)
         sent += e
 
@@ -113,12 +127,13 @@ def rank_program(g, core, T, topo):
     tot, qe, bt, sd, rs, negmu, nb = [T.sm[:, i:i + 1] for i in range(7)]
     for j in range(kk):
         v.wait_ge(sem["vr%d" % j], 1)
-    v.wait_ge(sem.aq, kk)
-    v.wait_ge(sem.arr, arrive)
-    a.wait_ge(sem.aq, kk)
-    a.wait_ge(sem.arr, arrive)
+    for q in (v, a):
+        if ne:
+            q.wait_ge(sem.ae, ne)
+        q.wait_ge(sem.aq, kk - ne)
+        q.wait_ge(sem.arr, arrive)
     if not direct:
-        v.tensor_copy(slot, T.mine[:, 0:2 * kk]).then_inc(sem.cp, 1)
+        v.tensor_copy(T.land[:, 2 * o:2 * (o + kk)], T.mine[:, 0:2 * kk]).then_inc(sem.cp, 1)
         v.wait_ge(sem.cp, 1)
         a.wait_ge(sem.cp, 1)
     v.tensor_reduce(tot, landA, X, add, negate=True).then_inc(sem.v1, 1)

@@ -6,9 +6,11 @@ EPS = 0.01
 MAXP = 8
 NE = 8
 EARLY = 1
+FB = 128
 
 SCRATCH = {
     "xb": ("sbuf", [128, 512], "float32"),
+    "zb": ("sbuf", [128, 512], "float32"),
     "yb": ("sbuf", [128, 512], "float32"),
     "junk": ("sbuf", [128, 512], "float32"),
     "junk2": ("sbuf", [128, 160], "float32"),
@@ -16,8 +18,8 @@ SCRATCH = {
     "mine": ("sbuf", [128, 16], "float32"),
     "sm": ("sbuf", [128, 8], "float32"),
 }
-SEMAPHORES = ["ld0", "ld1", "ld2", "ae", "aq", "arr", "snt", "cp", "a0", "a1", "a2", "a3", "v1", "v2", "v3", "vy", "ay",
-              "st"] + ["vr%d" % j for j in range(MAXP)]
+SEMAPHORES = ["ld0", "ld1", "ld2", "ae", "aq", "arr", "snt", "cp", "a0", "a1", "a2", "v1", "v2", "v3", "v4",
+              "vz0", "vz1", "vy0", "vy1", "ay0", "ay1", "st"] + ["vr%d" % j for j in range(MAXP)]
 
 
 def _layout(cnt):
@@ -124,7 +126,8 @@ def rank_program(g, core, T, topo):
 
     landA = T.land[:, 0:2 * npair:2]
     landQ = T.land[:, 1:2 * npair:2]
-    tot, qe, bt, sd, rs, negmu, nb = [T.sm[:, i:i + 1] for i in range(7)]
+    tot, qe, bt, sd, rv, negmu, vf = [T.sm[:, i:i + 1] for i in range(7)]
+    cb = float(w) / (float(nt) ** 3)
     for j in range(kk):
         v.wait_ge(sem["vr%d" % j], 1)
     for q in (v, a):
@@ -142,29 +145,34 @@ def rank_program(g, core, T, topo):
     a.wait_ge(sem.v1, 1)
     a.activation(T.junk2[:, 80:80 + npair], landA, F.Square, bias=tot, scale=float(npair),
                  accum_out=bt).then_inc(sem.a1, 1)
-    v.wait_ge(sem.v1, 1)
-    v.tensor_scalar(negmu, tot, -1.0 / nt, None, mult).then_inc(sem.v2, 1)
     a.wait_ge(sem.a0, 1)
     a.wait_ge(sem.a1, 1)
-    a.activation(sd, bt, F.Sqrt, bias=qe, scale=float(w) / (float(nt) ** 3)).then_inc(sem.a2, 1)
-    v.wait_ge(sem.a2, 1)
-    v.reciprocal(rs, sd).then_inc(sem.v3, 1)
+    a.activation(sd, bt, F.Sqrt, bias=qe, scale=cb).then_inc(sem.a2, 1)
 
-    na = ((n - w) // 2) // 4 * 4
-    if na < 32:
-        na = 0
-    nv = n - na
+    blocks = [(0, min(n, FB))] + ([(FB, n)] if n > FB else [])
+    v.wait_ge(sem.v1, 1)
+    v.tensor_scalar(negmu, tot, -1.0 / nt, None, mult).then_inc(sem.v2, 1)
+    v.wait_ge(sem.a0, 1)
+    v.wait_ge(sem.a1, 1)
+    v.tensor_scalar(vf, bt, cb, qe, mult, add).then_inc(sem.v4, 1)
+    v.wait_ge(sem.v4, 1)
+    v.reciprocal(rv, vf).then_inc(sem.v3, 1)
     v.wait_ge(sem.v2, 1)
     v.wait_ge(sem.v3, 1)
-    v.tensor_scalar(T.yb[:, 0:nv], T.xb[:, 0:nv], negmu, rs, add, mult).then_inc(sem.vy, 1)
-    s.wait_ge(sem.vy, 1)
-    if na:
-        a.wait_ge(sem.v2, 1)
-        a.wait_ge(sem.v3, 1)
-        a.activation(nb, negmu, F.Identity, scale=rs).then_inc(sem.a3, 1)
-        a.wait_ge(sem.a3, 1)
-        a.activation(T.yb[:, nv:n], T.xb[:, nv:n], F.Identity, bias=nb, scale=rs).then_inc(sem.ay, 1)
-        s.wait_ge(sem.ay, 1)
-    s.dma_start(T.y[:, 0:n], T.yb[:, 0:n]).then_inc(sem.st, 16)
-    s.wait_ge(sem.st, 16)
+    for i, (c0, c1) in enumerate(blocks):
+        v.tensor_scalar(T.zb[:, c0:c1], T.xb[:, c0:c1], negmu, rv, add, mult).then_inc(sem["vz%d" % i], 1)
+
+    v.wait_ge(sem.a2, 1)
+    a.wait_ge(sem.a2, 1)
+    for i, (c0, c1) in enumerate(blocks):
+        mid = (c0 + c1) // 2 if c1 - c0 >= 2 * w else c1
+        v.wait_ge(sem["vz%d" % i], 1)
+        v.tensor_scalar(T.yb[:, c0:mid], T.zb[:, c0:mid], sd, None, mult).then_inc(sem["vy%d" % i], 1)
+        s.wait_ge(sem["vy%d" % i], 1)
+        if mid < c1:
+            a.wait_ge(sem["vz%d" % i], 1)
+            a.activation(T.yb[:, mid:c1], T.zb[:, mid:c1], F.Identity, scale=sd).then_inc(sem["ay%d" % i], 1)
+            s.wait_ge(sem["ay%d" % i], 1)
+        s.dma_start(T.y[:, c0:c1], T.yb[:, c0:c1]).then_inc(sem.st, 16)
+    s.wait_ge(sem.st, 16 * len(blocks))
     g.wait_ge(sem.snt, sent)

@@ -10,16 +10,15 @@ FB = 128
 
 SCRATCH = {
     "xb": ("sbuf", [128, 512], "float32"),
-    "zb": ("sbuf", [128, 512], "float32"),
     "yb": ("sbuf", [128, 512], "float32"),
     "junk": ("sbuf", [128, 512], "float32"),
     "junk2": ("sbuf", [128, 160], "float32"),
     "land": ("sbuf", [128, 160], "float32"),
     "mine": ("sbuf", [128, 16], "float32"),
-    "sm": ("sbuf", [128, 8], "float32"),
+    "sm": ("sbuf", [128, 16], "float32"),
 }
-SEMAPHORES = ["ld0", "ld1", "ld2", "ae", "aq", "arr", "snt", "cp", "a0", "a1", "a2", "v1", "v2", "v3", "v4",
-              "vz0", "vz1", "vy0", "vy1", "ay0", "ay1", "st"] + ["vr%d" % j for j in range(MAXP)]
+SEMAPHORES = ["ld0", "ld1", "ld2", "ae", "aq", "arr", "snt", "cp", "e0", "e1", "e2", "a0", "a1", "a2", "a3", "a4",
+              "v1", "v2", "v3", "vy0", "vy1", "ay0", "ay1", "st"] + ["vr%d" % j for j in range(MAXP)]
 
 
 def _layout(cnt):
@@ -124,55 +123,61 @@ def rank_program(g, core, T, topo):
                            local_sem=sem.snt)
         sent += e
 
-    landA = T.land[:, 0:2 * npair:2]
-    landQ = T.land[:, 1:2 * npair:2]
-    tot, qe, bt, sd, rv, negmu, vf = [T.sm[:, i:i + 1] for i in range(7)]
-    cb = float(w) / (float(nt) ** 3)
-    for j in range(kk):
-        v.wait_ge(sem["vr%d" % j], 1)
+    tot, qe, bt, tq, sd, rs, negmu, nb, s0, si, c1, c2, c3 = [T.sm[:, i:i + 1] for i in range(13)]
     for q in (v, a):
         if ne:
             q.wait_ge(sem.ae, ne)
         q.wait_ge(sem.aq, kk - ne)
-        q.wait_ge(sem.arr, arrive)
+
+    a.activation(s0, stat[:, base + 1:base + 2], F.Sqrt, bias=EPS, scale=1.0 / (float(w) ** 3)).then_inc(sem.e0, 1)
+    v.wait_ge(sem.e0, 1)
+    v.reciprocal(si, s0).then_inc(sem.e1, 1)
+    v.wait_ge(sem.e1, 1)
+    v.tensor_scalar(c2, si, si, 1.0 / (float(w) * w * nt), mult, mult).then_inc(sem.e2, 1)
+    v.tensor_scalar(c3, si, si, EPS / npair, mult, mult).then_inc(sem.e2, 1)
+    v.tensor_scalar(c1, si, si, float(w) / (float(nt) ** 3), mult, mult).then_inc(sem.e2, 1)
+
+    landA = T.land[:, 0:2 * npair:2]
+    landQ = T.land[:, 1:2 * npair:2]
+    for j in range(kk):
+        v.wait_ge(sem["vr%d" % j], 1)
+    v.wait_ge(sem.arr, arrive)
+    a.wait_ge(sem.arr, arrive)
     if not direct:
         v.tensor_copy(T.land[:, 2 * o:2 * (o + kk)], T.mine[:, 0:2 * kk]).then_inc(sem.cp, 1)
         v.wait_ge(sem.cp, 1)
         a.wait_ge(sem.cp, 1)
     v.tensor_reduce(tot, landA, X, add, negate=True).then_inc(sem.v1, 1)
-    a.activation(T.junk2[:, 0:npair], landQ, F.Identity, bias=EPS / npair, scale=1.0 / (float(w) * w * nt),
-                 accum_out=qe).then_inc(sem.a0, 1)
+    a.wait_ge(sem.e2, 3)
+    a.activation(T.junk2[:, 0:npair], landQ, F.Identity, bias=c3, scale=c2, accum_out=qe).then_inc(sem.a0, 1)
     a.wait_ge(sem.v1, 1)
     a.activation(T.junk2[:, 80:80 + npair], landA, F.Square, bias=tot, scale=float(npair),
                  accum_out=bt).then_inc(sem.a1, 1)
     a.wait_ge(sem.a0, 1)
     a.wait_ge(sem.a1, 1)
-    a.activation(sd, bt, F.Sqrt, bias=qe, scale=cb).then_inc(sem.a2, 1)
-
-    blocks = [(0, min(n, FB))] + ([(FB, n)] if n > FB else [])
+    a.activation(tq, bt, F.Sqrt, bias=qe, scale=c1).then_inc(sem.a2, 1)
+    a.wait_ge(sem.a2, 1)
+    a.activation(sd, tq, F.Identity, scale=s0).then_inc(sem.a3, 1)
     v.wait_ge(sem.v1, 1)
     v.tensor_scalar(negmu, tot, -1.0 / nt, None, mult).then_inc(sem.v2, 1)
-    v.wait_ge(sem.a0, 1)
-    v.wait_ge(sem.a1, 1)
-    v.tensor_scalar(vf, bt, cb, qe, mult, add).then_inc(sem.v4, 1)
-    v.wait_ge(sem.v4, 1)
-    v.reciprocal(rv, vf).then_inc(sem.v3, 1)
+    v.wait_ge(sem.a3, 1)
+    v.reciprocal(rs, sd).then_inc(sem.v3, 1)
+
+    blocks = [(0, min(n, FB))] + ([(FB, n)] if n > FB else [])
     v.wait_ge(sem.v2, 1)
     v.wait_ge(sem.v3, 1)
-    for i, (c0, c1) in enumerate(blocks):
-        v.tensor_scalar(T.zb[:, c0:c1], T.xb[:, c0:c1], negmu, rv, add, mult).then_inc(sem["vz%d" % i], 1)
-
-    v.wait_ge(sem.a2, 1)
-    a.wait_ge(sem.a2, 1)
-    for i, (c0, c1) in enumerate(blocks):
-        mid = (c0 + c1) // 2 if c1 - c0 >= 2 * w else c1
-        v.wait_ge(sem["vz%d" % i], 1)
-        v.tensor_scalar(T.yb[:, c0:mid], T.zb[:, c0:mid], sd, None, mult).then_inc(sem["vy%d" % i], 1)
+    if n >= 2 * w:
+        a.wait_ge(sem.v2, 1)
+        a.wait_ge(sem.v3, 1)
+        a.activation(nb, negmu, F.Identity, scale=rs).then_inc(sem.a4, 1)
+        a.wait_ge(sem.a4, 1)
+    for i, (c0, c1_) in enumerate(blocks):
+        mid = (c0 + c1_) // 2 if c1_ - c0 >= 2 * w else c1_
+        v.tensor_scalar(T.yb[:, c0:mid], T.xb[:, c0:mid], negmu, rs, add, mult).then_inc(sem["vy%d" % i], 1)
         s.wait_ge(sem["vy%d" % i], 1)
-        if mid < c1:
-            a.wait_ge(sem["vz%d" % i], 1)
-            a.activation(T.yb[:, mid:c1], T.zb[:, mid:c1], F.Identity, scale=sd).then_inc(sem["ay%d" % i], 1)
+        if mid < c1_:
+            a.activation(T.yb[:, mid:c1_], T.xb[:, mid:c1_], F.Identity, bias=nb, scale=rs).then_inc(sem["ay%d" % i], 1)
             s.wait_ge(sem["ay%d" % i], 1)
-        s.dma_start(T.y[:, c0:c1], T.yb[:, c0:c1]).then_inc(sem.st, 16)
+        s.dma_start(T.y[:, c0:c1_], T.yb[:, c0:c1_]).then_inc(sem.st, 16)
     s.wait_ge(sem.st, 16 * len(blocks))
     g.wait_ge(sem.snt, sent)

import math
from concourse.bass import DstId, RemoteDMATransfer
from concourse.mybir import AluOpType, AxisListType, ActivationFunctionType

EPS = 0.01
MAXP = 8
NE = 8
EARLY = 1
FB = 128

SCRATCH = {
    "xb": ("sbuf", [128, 512], "float32"),
    "yb": ("sbuf", [128, 512], "float32"),
    "junk": ("sbuf", [128, 512], "float32"),
    "junk2": ("sbuf", [128, 160], "float32"),
    "land": ("sbuf", [128, 160], "float32"),
    "mine": ("sbuf", [128, 16], "float32"),
    "sm": ("sbuf", [128, 16], "float32"),
}
SEMAPHORES = ["ld0", "ld1", "ld2", "ae", "aq", "arr", "snt", "cp", "e0", "e1", "e2", "a0", "a1", "a2", "a3", "a4",
              "v1", "v2", "v3", "vy0", "vy1", "ay0", "ay1", "st"] + ["vr%d" % j for j in range(MAXP)]


def _layout(cnt):
    n = len(cnt)
    w = math.gcd(*cnt)
    k = [c // w for c in cnt]
    order = [r for r in range(n) if k[r] % 2 == 0] + sorted([r for r in range(n) if k[r] % 2], key=lambda r: k[r])
    off, p = {}, 0
    for r in order:
        off[r] = p
        p += k[r]
    return w, k, off, p


def _parts(kk):
    if kk <= EARLY:
        return [0]
    if kk < 4:
        return [0, EARLY]
    return [0, EARLY, kk - kk // 4]


def _plan(s, cnt, k, cores, topo):
    n = len(cnt)
    dests = sorted([d for d in range(n) if d != s], key=lambda d: (-cnt[d], (d - s) % n))
    ne = EARLY if k[s] > EARLY else 0

    def engines(grp):
        m = -1
        for d in grp:
            if not topo.may_write(cores[s], cores[d]):
                raise ValueError("rank %d may not write to rank %d" % (s, d))
            m &= topo.mask(cores[s], cores[d])
        bits = [b for b in range(16) if (m >> b) & 1]
        e = 1
        while e * 2 <= min(len(bits), NE):
            e *= 2
        return sum(1 << b for b in bits[:e]), e

    if not ne:
        return 0, [engines(dests) + (dests, 0, k[s])]
    return ne, [engines(dests[-1:]) + (dests[-1:], 0, ne),
                engines(dests[:-1]) + (dests[:-1], 0, k[s]),
                engines(dests[-1:]) + (dests[-1:], ne, k[s])]


def rank_program(g, core, T, topo):
    rank = T.rank_of(core)
    if rank is None:
        return
    cnt = [int(c) for c in T.tables["CNT"]]
    cores = [int(c) for c in T.cores]
    nr = len(cnt)
    nt = sum(cnt)
    w, k, off, npair = _layout(cnt)
    n, kk, o = cnt[rank], k[rank], off[rank]
    sem = T.sem
    v, a, s = g.vector, g.scalar, g.sync
    add, mult = AluOpType.add, AluOpType.mult
    X = AxisListType.X
    F = ActivationFunctionType

    direct = o % 2 == 0 and ((o + kk) % 2 == 0 or o + kk == npair)
    stat, base = (T.land, 2 * o) if direct else (T.mine, 0)
    ne, calls = _plan(rank, cnt, k, cores, topo)
    arrive = sum(c[1] for q in range(nr) if q != rank for c in _plan(q, cnt, k, cores, topo)[1] if rank in c[2])

    parts = _parts(kk)
    for i, p0 in enumerate(parts):
        p1 = parts[i + 1] if i + 1 < len(parts) else kk
        s.dma_start(T.xb[:, p0 * w:p1 * w], T.x[:, p0 * w:p1 * w]).then_inc(sem["ld%d" % i], 16)

    for j in range(kk):
        if j in parts:
            v.wait_ge(sem["ld%d" % parts.index(j)], 16)
            a.wait_ge(sem["ld%d" % parts.index(j)], 16)
        A = stat[:, base + 2 * j:base + 2 * j + 1]
        Q = stat[:, base + 2 * j + 1:base + 2 * j + 2]
        xs = T.xb[:, j * w:(j + 1) * w]
        v.tensor_reduce(A, xs, X, add, negate=True).then_inc(sem["vr%d" % j], 1)
        a.wait_ge(sem["vr%d" % j], 1)
        a.activation(T.junk[:, j * w:(j + 1) * w], xs, F.Square, bias=A, scale=float(w),
                     accum_out=Q).then_inc(sem.ae if j < ne else sem.aq, 1)

    sent = 0
    for i, (m, e, grp, p0, p1) in enumerate(calls):
        if i == 0 and ne:
            for j in range(ne):
                g.wait_ge(sem["vr%d" % j], 1)
            g.wait_ge(sem.ae, ne)
        if i == (1 if ne else 0):
            for j in range(ne, kk):
                g.wait_ge(sem["vr%d" % j], 1)
            g.wait_ge(sem.aq, kk - ne)
        ids = []
        for d in grp:
            rid, pid, _ = topo.addr(cores[d])
            ids.append(DstId(rid=rid, pnc=pid))
        g.remote_dma_fused([RemoteDMATransfer(dst_ids=ids, dma_engine_mask=m, remote_sem=sem.arr,
                                              srcs=[stat[:, base + 2 * p0:base + 2 * p1]],
                                              dsts=[T.land[:, 2 * (o + p0):2 * (o + p1)] for _ in grp])],
                           local_sem=sem.snt)
        sent += e

    tot, qe, bt, tq, sd, rs, negmu, nb, s0, si, c1, c2, c3 = [T.sm[:, i:i + 1] for i in range(13)]
    for q in (v, a):
        if ne:
            q.wait_ge(sem.ae, ne)
        q.wait_ge(sem.aq, kk - ne)

    a.activation(s0, stat[:, base + 1:base + 2], F.Sqrt, bias=EPS, scale=1.0 / (float(w) ** 3)).then_inc(sem.e0, 1)
    v.wait_ge(sem.e0, 1)
    v.reciprocal(si, s0).then_inc(sem.e1, 1)
    v.wait_ge(sem.e1, 1)
    v.tensor_scalar(c2, si, si, 1.0 / (float(w) * w * nt), mult, mult).then_inc(sem.e2, 1)
    v.tensor_scalar(c3, si, si, EPS / npair, mult, mult).then_inc(sem.e2, 1)
    v.tensor_scalar(c1, si, si, float(w) / (float(nt) ** 3), mult, mult).then_inc(sem.e2, 1)

    landA = T.land[:, 0:2 * npair:2]
    landQ = T.land[:, 1:2 * npair:2]
    for j in range(kk):
        v.wait_ge(sem["vr%d" % j], 1)
    v.wait_ge(sem.arr, arrive)
    a.wait_ge(sem.arr, arrive)
    if not direct:
        v.tensor_copy(T.land[:, 2 * o:2 * (o + kk)], T.mine[:, 0:2 * kk]).then_inc(sem.cp, 1)
        v.wait_ge(sem.cp, 1)
        a.wait_ge(sem.cp, 1)
    v.tensor_reduce(tot, landA, X, add, negate=True).then_inc(sem.v1, 1)
    a.wait_ge(sem.e2, 3)
    a.activation(T.junk2[:, 0:npair], landQ, F.Identity, bias=c3, scale=c2, accum_out=qe).then_inc(sem.a0, 1)
    a.wait_ge(sem.v1, 1)
    a.activation(T.junk2[:, 80:80 + npair], landA, F.Square, bias=tot, scale=float(npair),
                 accum_out=bt).then_inc(sem.a1, 1)
    a.wait_ge(sem.a0, 1)
    a.wait_ge(sem.a1, 1)
    a.activation(tq, bt, F.Sqrt, bias=qe, scale=c1).then_inc(sem.a2, 1)
    a.wait_ge(sem.a2, 1)
    a.activation(sd, tq, F.Identity, scale=s0).then_inc(sem.a3, 1)
    v.wait_ge(sem.v1, 1)
    v.tensor_scalar(negmu, tot, -1.0 / nt, None, mult).then_inc(sem.v2, 1)
    v.wait_ge(sem.a3, 1)
    v.reciprocal(rs, sd).then_inc(sem.v3, 1)

    blocks = [(0, min(n, FB))] + ([(FB, n)] if n > FB else [])
    v.wait_ge(sem.v2, 1)
    v.wait_ge(sem.v3, 1)
    if n >= 2 * w:
        a.wait_ge(sem.v2, 1)
        a.wait_ge(sem.v3, 1)
        a.activation(nb, negmu, F.Identity, scale=rs).then_inc(sem.a4, 1)
        a.wait_ge(sem.a4, 1)
    for i, (c0, c1_) in enumerate(blocks):
        mid = (c0 + c1_) // 2 if c1_ - c0 >= 2 * w else c1_
        v.tensor_scalar(T.yb[:, c0:mid], T.xb[:, c0:mid], negmu, rs, add, mult).then_inc(sem["vy%d" % i], 1)
        s.wait_ge(sem["vy%d" % i], 1)
        if mid < c1_:
            a.activation(T.yb[:, mid:c1_], T.xb[:, mid:c1_], F.Identity, bias=nb, scale=rs).then_inc(sem["ay%d" % i], 1)
            s.wait_ge(sem["ay%d" % i], 1)
        s.dma_start(T.y[:, c0:c1_], T.yb[:, c0:c1_]).then_inc(sem.st, 16)
    s.wait_ge(sem.st, 16 * len(blocks))
    g.wait_ge(sem.snt, sent)
